import numpy as np
import ml_dtypes


def mxq(x, axis, fmt="e4m3"):
    dtype, down = {"e4m3": (ml_dtypes.float8_e4m3fn, 7), "e5m2": (ml_dtypes.float8_e5m2, 14)}[fmt]
    v = np.moveaxis(np.asarray(x, np.float32).astype(ml_dtypes.bfloat16).astype(np.float64), axis, -1)
    blocks = v.reshape(v.shape[:-1] + (-1, 32))
    amax = np.abs(blocks).max(-1, keepdims=True)
    byte = np.maximum(np.where(amax > 0, np.frexp(amax)[1] - 1 + 127, 0) - down, 1)
    scale = np.exp2(byte - 127.0)
    codes = (blocks / scale).astype(np.float32).astype(dtype).astype(np.float64)
    return np.moveaxis((codes * scale).reshape(v.shape), -1, axis)


WIDE = False


def mx_kscale(k):
    if not WIDE:
        return np.ones(k)
    levels = np.array([10, -10, 5, -5, 0])
    if k % 512:
        return np.exp2(np.random.permutation(np.resize(levels, k // 32))).repeat(32)
    a = np.empty((k // 512, 16))
    for p in range(k // 512):
        a[p, :8] = np.random.permutation(np.resize(levels, 8))
        for g in range(8):
            far = levels[np.abs(levels - a[p, g]) >= 10]
            a[p, g + 8] = far[np.random.randint(len(far))]
    return np.exp2(a.ravel()).repeat(32)


def f64(x):
    return np.asarray(x).astype(np.float64)


def striped8(idx):
    return np.asarray(idx).reshape(8, -1, 16).transpose(0, 2, 1).reshape(128, -1).astype(np.uint16)


def unstriped8(offs):
    return offs.reshape(8, 16, -1).transpose(0, 2, 1).reshape(8, -1).astype(np.int64)


def pick8(x, idx, run):
    r = np.arange(len(x))
    return x[r[:, None], idx[r % (8 * run) // run]]


E2M1 = np.array([0.0, 0.5, 1.0, 1.5, 2.0, 3.0, 4.0, 6.0, -0.0, -0.5, -1.0, -1.5, -2.0, -3.0, -4.0, -6.0])


def pack_weight(w, fmt):
    k, n = w.shape
    w = f64(np.asarray(w, np.float32).astype(ml_dtypes.bfloat16)).reshape(k // 32, 32, n)
    amax = np.abs(w).max(1)
    if fmt == "e4m3":
        byte = np.frexp(amax)[1] - 1 + 127 - 7
    else:
        mant, ex = np.frexp(amax / 6.0)
        byte = np.where(mant > 0.5, ex, ex - 1) + 127
    byte = np.clip(np.where(amax > 0, byte, 1), 1, 254)
    scaled = (w * np.exp2(127.0 - byte)[:, None, :]).reshape(k, n).astype(np.float32)
    by_word = np.ascontiguousarray(scaled.reshape(k // 512, 128, 4, n).transpose(0, 1, 3, 2))
    if fmt == "e4m3":
        words = by_word.astype(ml_dtypes.float8_e4m3fn).view(np.uint8)
    else:
        c = by_word.astype(ml_dtypes.float4_e2m1fn).view(np.uint8) & 0xF
        words = (c[..., 0::2] | (c[..., 1::2] << 4)).reshape(k // 512, 128, 2 * n)
    return np.ascontiguousarray(words), np.ascontiguousarray(byte.astype(np.uint8).reshape(k // 512, 16, n))


def unpack_weight(words, scales, fmt):
    g, _, n = scales.shape
    words = np.ascontiguousarray(words).reshape(g, 128, n, -1)
    if fmt == "e4m3":
        vals = words.view(ml_dtypes.float8_e4m3fn).astype(np.float64)
    else:
        nib = np.empty((g, 128, n, 4), np.uint8)
        nib[..., 0::2] = words & 0xF
        nib[..., 1::2] = words >> 4
        vals = E2M1[nib]
    vals = vals * np.repeat(np.exp2(scales.astype(np.float64) - 127.0), 8, axis=1)[..., None]
    return vals.transpose(0, 1, 3, 2).reshape(g * 512, n)


def bf(x):
    return np.asarray(x, np.float32).astype(ml_dtypes.bfloat16)


def planes(Y):
    r, m = Y.shape
    b = f64(bf(Y)).reshape(r // 32, 32, m)
    amax = np.abs(b).max(1)
    byte = np.clip(np.where(amax > 0, np.frexp(amax)[1] - 1 + 127 - 7, 1), 1, 254)
    codes = (b * np.exp2(127.0 - byte)[:, None, :]).reshape(r, m).astype(np.float32).astype(ml_dtypes.float8_e4m3fn).view(np.uint8)
    words = codes.reshape(r // 512, 128, 4, m).transpose(0, 1, 3, 2)
    return np.ascontiguousarray(words), np.ascontiguousarray(byte.astype(np.uint8).reshape(r // 512, 16, m))


K, T, J, N = 1024, 1024, 512, 512


def setup_inputs():
    n = np.random.standard_normal
    idx = np.stack([np.random.permutation(T)[:J] for _ in range(8)])
    idx2 = np.stack([np.random.permutation(T)[:J] for _ in range(8)])
    fk = mx_kscale(K)
    wp = pack_weight(n((K, N)) * 1 / np.sqrt(K) * fk[:, None], "e4m3")
    return {
        "xf": (n((K, T))).astype(np.float32),
        "fk": (np.random.uniform(0.5, 2.0, (K, 1)) / fk[:, None]).astype(np.float32),
        "w_words": wp[0],
        "w_scales": wp[1],
        "rw": (np.random.uniform(0.5, 2.0, (1, J))).astype(np.float32),
        "offs": striped8(idx),
        "offs2": striped8(idx2),
    }


def reference(xf, fk, w_words, w_scales, rw, offs, offs2):
    idx = unstriped8(offs)
    idx2 = unstriped8(offs2)
    wu = unpack_weight(w_words, w_scales, "e4m3")
    u = np.maximum(pick8(f64(xf), idx, 64), pick8(f64(xf), idx2, 64)) * f64(fk)
    uq = mxq(u, 0, "e4m3")
    p = wu.T @ uq
    y = p * f64(rw)
    words, scales = planes(y)
    return y, words, scales

@@ -1,0 +1,185 @@
+from contextlib import ExitStack
+
+import concourse.mybir as mybir
+
+K, T, J, N = 1024, 1024, 512, 512
+FLOPS = 2 * K * J * N
+
+F32 = mybir.dt.float32
+BF16 = mybir.dt.bfloat16
+I32 = mybir.dt.int32
+U32 = mybir.dt.uint32
+U16 = mybir.dt.uint16
+U8 = mybir.dt.uint8
+FP8X4 = mybir.dt.float8_e4m3fn_x4
+COPY = mybir.ActivationFunctionType.Copy
+MAX = mybir.AluOpType.max
+MULT = mybir.AluOpType.mult
+
+P = 128
+PACK = 4
+PASSES = K // (P * PACK)
+NPL = PASSES * PACK
+HALF = J // 2
+QUART = 128
+
+
+def tile_list_head_larger_inputs_pl_kernel(tc, xf, fk, w_words, w_scales, rw, offs, offs2, out_0, out_1, out_2):
+    nc = tc.nc
+    with ExitStack() as ctx:
+        keep = ctx.enter_context(tc.tile_pool(name="keep", bufs=1))
+        psum = ctx.enter_context(tc.psum_pool(name="psum", bufs=1))
+
+        list1 = keep.tile([P, J // 16], U16, name="list1")
+        list2 = keep.tile([P, J // 16], U16, name="list2")
+        x = [keep.tile([P, T], F32, name=f"x{s}") for s in range(NPL)]
+        fk_sb = keep.tile([P, PASSES, PACK], F32, name="fk_sb")
+        rw_sb = keep.tile([P, J], F32, name="rw_sb")
+        w_raw = [keep.tile([P, N], U32, name=f"w_raw{a}") for a in range(PASSES)]
+        w_raw_planes = keep.tile([P, N], U8, name="w_raw_planes")
+        w_codes = [keep.tile([P, PACK, P], U32, name=f"w_codes{a}", align_bytes=64) for a in range(PASSES)]
+        w_planes = keep.tile([P, PACK, P], U8, name="w_planes", align_bytes=64)
+
+        x_rows = xf.rearrange("(a p i) t -> a i p t", a=PASSES, i=PACK)
+
+        def load_x(s):
+            nc.sync.dma_start(x[s][:], x_rows[s // PACK, s % PACK])
+
+        def load_w(a):
+            nc.sync.dma_start(w_raw[a][:].bitcast(I32), w_words[a].rearrange("p n r -> p (n r)").bitcast(I32))
+
+        nc.vector.memset(w_raw_planes[:].bitcast(U32), 0)
+
+        load_x(0)
+        nc.sync.dma_start(list1[:], offs)
+        nc.sync.dma_start(list2[:], offs2)
+        load_x(1)
+        nc.sync.dma_start(fk_sb[:], fk.rearrange("(a p i) o -> p a (i o)", a=PASSES, i=PACK))
+        for s in range(2, NPL):
+            load_x(s)
+        for a in range(PASSES):
+            load_w(a)
+        for q in range(4):
+            nc.sync.dma_start(
+                w_raw_planes[32 * q : 32 * q + 4 * PASSES, :].bitcast(I32),
+                w_scales[:, 4 * q : 4 * q + 4, :].bitcast(I32),
+            )
+        nc.sync.dma_start(rw_sb[:], rw[0].partition_broadcast(P))
+
+        pick1 = {(h, s): keep.tile([P, HALF], F32, name=f"pick1_{h}{s}") for h in range(2) for s in range(NPL)}
+        ring2 = [keep.tile([P, HALF], F32, name=f"pick2_{r}") for r in range(2)]
+        larger = {(h, s): keep.tile([P, HALF], F32, name=f"larger{h}{s}") for h in range(2) for s in range(NPL)}
+        u_bf = [keep.tile([P, PASSES, HALF, PACK], BF16, name=f"u_bf{h}", align_bytes=64) for h in range(2)]
+        u_codes = {}
+        u_planes = {}
+        for key, width in (((0, 0), 2 * HALF), ((1, 0), HALF), ((1, 1), HALF)):
+            u_codes[key] = keep.tile([P, width], U32, name=f"u_codes{key[0]}{key[1]}", align_bytes=64)
+            u_planes[key] = keep.tile([P, width], U8, name=f"u_planes{key[0]}{key[1]}", align_bytes=64)
+        acc = [psum.tile([P, PACK, QUART], F32, name=f"acc{c}") for c in range(4)]
+        y_sb = [keep.tile([P, PACK, QUART], F32, name=f"y_sb{c}") for c in range(4)]
+        y_bf = keep.tile([P, J, PACK], BF16, name="y_bf", align_bytes=64)
+        y_codes = keep.tile([P, J], U32, name="y_codes", align_bytes=64)
+        y_planes = keep.tile([P, J], U8, name="y_planes", align_bytes=64)
+
+        out_rows = out_0.rearrange("(p t) j -> p t j", t=PACK)
+        out_words = out_1[0].rearrange("p j r -> p (j r)").bitcast(I32)
+
+        def deal_w():
+            for a in range(PASSES):
+                nc.vector.tensor_copy(w_codes[a][:], w_raw[a][:].rearrange("p (m t) -> p t m", t=PACK))
+            nc.vector.tensor_copy(w_planes[:], w_raw_planes[:].rearrange("p (m t) -> p t m", t=PACK))
+
+        def gather(dst, lst, h, s):
+            cols = slice(h * HALF // 16, (h + 1) * HALF // 16)
+            nc.vector.tensor_copy(dst[:], x[s][:].indirect(lst[:, cols]))
+
+        def combine(h, s, second):
+            a, i = divmod(s, PACK)
+            m = larger[h, s]
+            nc.vector.tensor_tensor(m[:], pick1[h, s][:], second[:], MAX)
+            nc.scalar.activation(u_bf[h][:, a, :, i], m[:], COPY, scale=fk_sb[:, a, i : i + 1])
+
+        def quantise_u(key, src):
+            nc.vector.quantize_mx(out=u_codes[key][:].bitcast(FP8X4), scales=u_planes[key][:], in_=src)
+
+        def multiply(c, a, key, col0):
+            cols = slice(col0, col0 + QUART)
+            for t in range(PACK):
+                nc.tensor.matmul_mx(
+                    out=acc[c][:, t, :],
+                    lhsT=w_codes[a][:, t, :].bitcast(FP8X4),
+                    lhsT_scale=w_planes[4 * a : P, t, :],
+                    rhs=u_codes[key][:, cols].bitcast(FP8X4),
+                    rhs_scale=u_planes[key][:, cols],
+                    start=(a == 0 and t == 0),
+                    stop=(a == PASSES - 1 and t == PACK - 1),
+                )
+
+        def weigh(c):
+            cols = slice(c * QUART, (c + 1) * QUART)
+            nc.vector.tensor_tensor(y_sb[c][:], acc[c][:], rw_sb[:, cols].unsqueeze(1).to_broadcast([P, PACK, QUART]), MULT)
+            nc.sync.dma_start(out_rows[:, :, cols], y_sb[c][:])
+
+        def round_y(c):
+            cols = slice(c * QUART, (c + 1) * QUART)
+            nc.scalar.copy(y_bf[:, cols, :], y_sb[c][:].rearrange("p t j -> p j t"))
+
+        def weigh_and_round(c):
+            cols = slice(c * QUART, (c + 1) * QUART)
+            nc.vector.tensor_tensor(
+                y_bf[:, cols, :],
+                acc[c][:].rearrange("p t j -> p j t"),
+                rw_sb[:, cols].unsqueeze(2).to_broadcast([P, QUART, PACK]),
+                MULT,
+            )
+
+        def pack(c0, c1):
+            cols = slice(c0 * QUART, c1 * QUART)
+            nc.vector.quantize_mx(
+                out=y_codes[:, cols].bitcast(FP8X4),
+                scales=y_planes[:, cols],
+                in_=y_bf[:, cols, :].rearrange("p j t -> p (j t)"),
+            )
+
+        for s in range(NPL):
+            gather(pick1[0, s], list1, 0, s)
+            gather(ring2[0], list2, 0, s)
+            gather(pick1[1, s], list1, 1, s)
+            combine(0, s, ring2[0])
+        deal_w()
+
+        last = NPL - 1
+        order = [last] + list(range(last))
+        second = {last: ring2[1], 0: ring2[0], 1: pick1[0, last]}
+        for n in range(3, NPL):
+            second[order[n]] = second[order[n - 3]]
+        for n, s in enumerate(order):
+            gather(second[s], list2, 1, s)
+            if n > 0:
+                combine(1, order[n - 1], second[order[n - 1]])
+            if n == 1:
+                quantise_u((0, 0), u_bf[0][:].rearrange("p a j i -> p (a j i)"))
+                for c in range(2):
+                    for a in range(PASSES):
+                        multiply(c, a, (0, 0), a * HALF + c * QUART)
+            if n == 6:
+                quantise_u((1, 0), u_bf[1][:, 0].rearrange("p j i -> p (j i)"))
+                for c in range(2):
+                    multiply(2 + c, 0, (1, 0), c * QUART)
+        combine(1, order[-1], second[order[-1]])
+        quantise_u((1, 1), u_bf[1][:, 1].rearrange("p j i -> p (j i)"))
+        for c in range(2):
+            multiply(2 + c, 1, (1, 1), c * QUART)
+        for c in range(3):
+            weigh(c)
+            round_y(c)
+        weigh(3)
+        weigh_and_round(3)
+        pack(0, 2)
+        nc.sync.dma_start(out_words[:, 0:HALF], y_codes[:, 0:HALF].bitcast(I32))
+        pack(2, 3)
+        pack(3, 4)
+        nc.sync.dma_start(out_words[:, HALF:J], y_codes[:, HALF:J].bitcast(I32))
+        for q in range(4):
+            eng = nc.sync if q % 2 == 0 else nc.scalar
+            eng.dma_start(out_2[0, 4 * q : 4 * q + 4, :].bitcast(I32), y_planes[32 * q : 32 * q + 4, :].bitcast(I32))

@@ -69,10 +69,14 @@ def tile_list_head_larger_inputs_pl_kernel(tc, xf, fk, w_words, w_scales, rw, of
         pick1 = {(h, s): keep.tile([P, HALF], F32, name=f"pick1_{h}{s}") for h in range(2) for s in range(NPL)}
         ring2 = [keep.tile([P, HALF], F32, name=f"pick2_{r}") for r in range(2)]
         larger = {(h, s): keep.tile([P, HALF], F32, name=f"larger{h}{s}") for h in range(2) for s in range(NPL)}
-        u_bf = [keep.tile([P, PASSES, HALF, PACK], BF16, name=f"u_bf{h}", align_bytes=64) for h in range(2)]
+        u_bf_a = keep.tile([P, PASSES, HALF, PACK], BF16, name="u_bf_a", align_bytes=64)
+        u_bf_b = [keep.tile([P, HALF, PACK], BF16, name=f"u_bf_b{a}", align_bytes=64) for a in range(PASSES)]
+        u_bf = {(0, a): u_bf_a[:, a] for a in range(PASSES)}
+        for a in range(PASSES):
+            u_bf[1, a] = u_bf_b[a][:]
         u_codes = {}
         u_planes = {}
-        for key, width in (((0, 0), 2 * HALF), ((1, 0), HALF), ((1, 1), HALF)):
+        for key, width in (((0, 0), 2 * HALF), ((1, 0), HALF), ((1, 1), QUART), ((1, 2), QUART)):
             u_codes[key] = keep.tile([P, width], U32, name=f"u_codes{key[0]}{key[1]}", align_bytes=64)
             u_planes[key] = keep.tile([P, width], U8, name=f"u_planes{key[0]}{key[1]}", align_bytes=64)
         acc = [psum.tile([P, PACK, QUART], F32, name=f"acc{c}") for c in range(4)]
@@ -86,18 +90,21 @@ def tile_list_head_larger_inputs_pl_kernel(tc, xf, fk, w_words, w_scales, rw, of
 
         def deal_w():
             for a in range(PASSES):
-                nc.vector.tensor_copy(w_codes[a][:], w_raw[a][:].rearrange("p (m t) -> p t m", t=PACK))
-            nc.vector.tensor_copy(w_planes[:], w_raw_planes[:].rearrange("p (m t) -> p t m", t=PACK))
+                nc.gpsimd.tensor_copy(
+                    w_codes[a][:].rearrange("p t (c i) -> p c t i", i=4),
+                    w_raw[a][:].rearrange("p (c i t) -> p c t i", i=4, t=PACK),
+                )
+            nc.gpsimd.tensor_copy(w_planes[:], w_raw_planes[:].rearrange("p (m t) -> p t m", t=PACK))
 
         def gather(dst, lst, h, s):
             cols = slice(h * HALF // 16, (h + 1) * HALF // 16)
             nc.vector.tensor_copy(dst[:], x[s][:].indirect(lst[:, cols]))
 
-        def combine(h, s, second):
+        def combine(h, s, second, cols=slice(0, HALF)):
             a, i = divmod(s, PACK)
             m = larger[h, s]
-            nc.vector.tensor_tensor(m[:], pick1[h, s][:], second[:], MAX)
-            nc.scalar.activation(u_bf[h][:, a, :, i], m[:], COPY, scale=fk_sb[:, a, i : i + 1])
+            nc.vector.tensor_tensor(m[:, cols], pick1[h, s][:, cols], second[:, cols], MAX)
+            nc.scalar.activation(u_bf[h, a][:, cols, i], m[:, cols], COPY, scale=fk_sb[:, a, i : i + 1])
 
         def quantise_u(key, src):
             nc.vector.quantize_mx(out=u_codes[key][:].bitcast(FP8X4), scales=u_planes[key][:], in_=src)
@@ -115,21 +122,31 @@ def tile_list_head_larger_inputs_pl_kernel(tc, xf, fk, w_words, w_scales, rw, of
                     stop=(a == PASSES - 1 and t == PACK - 1),
                 )
 
-        def weigh(c):
+        def weigh(c, pieces):
             cols = slice(c * QUART, (c + 1) * QUART)
-            nc.vector.tensor_tensor(y_sb[c][:], acc[c][:], rw_sb[:, cols].unsqueeze(1).to_broadcast([P, PACK, QUART]), MULT)
+            rows = PACK // pieces
+            for t in range(0, PACK, rows):
+                nc.vector.tensor_tensor(
+                    y_sb[c][:, t : t + rows, :],
+                    acc[c][:, t : t + rows, :],
+                    rw_sb[:, cols].unsqueeze(1).to_broadcast([P, rows, QUART]),
+                    MULT,
+                )
             nc.sync.dma_start(out_rows[:, :, cols], y_sb[c][:])
 
         def round_y(c):
             cols = slice(c * QUART, (c + 1) * QUART)
-            nc.scalar.copy(y_bf[:, cols, :], y_sb[c][:].rearrange("p t j -> p j t"))
+            nc.scalar.copy(
+                y_bf[:, cols, :].rearrange("p (c i) t -> p c t i", i=4),
+                y_sb[c][:].rearrange("p t (c i) -> p c t i", i=4),
+            )
 
         def weigh_and_round(c):
             cols = slice(c * QUART, (c + 1) * QUART)
             nc.vector.tensor_tensor(
-                y_bf[:, cols, :],
-                acc[c][:].rearrange("p t j -> p j t"),
-                rw_sb[:, cols].unsqueeze(2).to_broadcast([P, QUART, PACK]),
+                y_bf[:, cols, :].rearrange("p (c i) t -> p c t i", i=4),
+                acc[c][:].rearrange("p t (c i) -> p c t i", i=4),
+                rw_sb[:, cols].rearrange("p (c i) -> p c i", i=4).unsqueeze(2).to_broadcast([P, QUART // 4, PACK, 4]),
                 MULT,
             )
 
@@ -151,35 +168,41 @@ def tile_list_head_larger_inputs_pl_kernel(tc, xf, fk, w_words, w_scales, rw, of
         last = NPL - 1
         order = [last] + list(range(last))
         second = {last: ring2[1], 0: ring2[0], 1: pick1[0, last]}
-        for n in range(3, NPL):
+        for n in range(3, last):
             second[order[n]] = second[order[n - 3]]
-        for n, s in enumerate(order):
+        second[order[last]] = second[order[last - 2]]
+        for n, s in enumerate(order[:last]):
             gather(second[s], list2, 1, s)
             if n > 0:
                 combine(1, order[n - 1], second[order[n - 1]])
             if n == 1:
-                quantise_u((0, 0), u_bf[0][:].rearrange("p a j i -> p (a j i)"))
+                quantise_u((0, 0), u_bf_a[:].rearrange("p a j i -> p (a j i)"))
                 for c in range(2):
                     for a in range(PASSES):
                         multiply(c, a, (0, 0), a * HALF + c * QUART)
             if n == 6:
-                quantise_u((1, 0), u_bf[1][:, 0].rearrange("p j i -> p (j i)"))
+                quantise_u((1, 0), u_bf[1, 0].rearrange("p j i -> p (j i)"))
                 for c in range(2):
                     multiply(2 + c, 0, (1, 0), c * QUART)
-        combine(1, order[-1], second[order[-1]])
-        quantise_u((1, 1), u_bf[1][:, 1].rearrange("p j i -> p (j i)"))
+        combine(1, order[last - 1], second[order[last - 1]])
+        gather(second[order[last]], list2, 1, order[last])
+        for d in range(2):
+            combine(1, order[last], second[order[last]], slice(d * QUART, (d + 1) * QUART))
+        for d in range(2):
+            quantise_u((1, 1 + d), u_bf[1, 1][:, d * QUART : (d + 1) * QUART, :].rearrange("p j i -> p (j i)"))
+            multiply(2 + d, 1, (1, 1 + d), 0)
         for c in range(2):
-            multiply(2 + c, 1, (1, 1), c * QUART)
-        for c in range(3):
-            weigh(c)
+            weigh(c, 2)
             round_y(c)
-        weigh(3)
-        weigh_and_round(3)
         pack(0, 2)
         nc.sync.dma_start(out_words[:, 0:HALF], y_codes[:, 0:HALF].bitcast(I32))
+        weigh(2, 1)
+        round_y(2)
+        weigh_and_round(3)
+        weigh(3, 1)
         pack(2, 3)
         pack(3, 4)
-        nc.sync.dma_start(out_words[:, HALF:J], y_codes[:, HALF:J].bitcast(I32))
+        nc.scalar.dma_start(out_words[:, HALF:J], y_codes[:, HALF:J].bitcast(I32))
         for q in range(4):
             eng = nc.sync if q % 2 == 0 else nc.scalar
             eng.dma_start(out_2[0, 4 * q : 4 * q + 4, :].bitcast(I32), y_planes[32 * q : 32 * q + 4, :].bitcast(I32))

@@ -66,9 +66,10 @@ def tile_list_head_larger_inputs_pl_kernel(tc, xf, fk, w_words, w_scales, rw, of
             )
         nc.sync.dma_start(rw_sb[:], rw[0].partition_broadcast(P))
 
-        pick1 = {(h, s): keep.tile([P, HALF], F32, name=f"pick1_{h}{s}") for h in range(2) for s in range(NPL)}
-        ring2 = [keep.tile([P, HALF], F32, name=f"pick2_{r}") for r in range(2)]
-        larger = {(h, s): keep.tile([P, HALF], F32, name=f"larger{h}{s}") for h in range(2) for s in range(NPL)}
+        pick1 = keep.tile([P, NPL, J], F32, name="pick1")
+        pick2_a = keep.tile([P, NPL, HALF], F32, name="pick2_a")
+        spare = keep.tile([P, HALF], F32, name="spare")
+        larger = [keep.tile([P, NPL, HALF], F32, name=f"larger{h}") for h in range(2)]
         u_bf_a = keep.tile([P, PASSES, HALF, PACK], BF16, name="u_bf_a", align_bytes=64)
         u_bf_b = [keep.tile([P, HALF, PACK], BF16, name=f"u_bf_b{a}", align_bytes=64) for a in range(PASSES)]
         u_bf = {(0, a): u_bf_a[:, a] for a in range(PASSES)}
@@ -79,7 +80,10 @@ def tile_list_head_larger_inputs_pl_kernel(tc, xf, fk, w_words, w_scales, rw, of
         for key, width in (((0, 0), 2 * HALF), ((1, 0), HALF), ((1, 1), QUART), ((1, 2), QUART)):
             u_codes[key] = keep.tile([P, width], U32, name=f"u_codes{key[0]}{key[1]}", align_bytes=64)
             u_planes[key] = keep.tile([P, width], U8, name=f"u_planes{key[0]}{key[1]}", align_bytes=64)
-        acc = [psum.tile([P, PACK, QUART], F32, name=f"acc{c}") for c in range(4)]
+        banks = {0: 1, 1: 1, 2: 2, 3: 1}
+        acc = {
+            (c, b): psum.tile([P, PACK // banks[c], QUART], F32, name=f"acc{c}{b}") for c in range(4) for b in range(banks[c])
+        }
         y_sb = [keep.tile([P, PACK, QUART], F32, name=f"y_sb{c}") for c in range(4)]
         y_bf = keep.tile([P, J, PACK], BF16, name="y_bf", align_bytes=64)
         y_codes = keep.tile([P, J], U32, name="y_codes", align_bytes=64)
@@ -96,58 +100,55 @@ def tile_list_head_larger_inputs_pl_kernel(tc, xf, fk, w_words, w_scales, rw, of
                 )
             nc.gpsimd.tensor_copy(w_planes[:], w_raw_planes[:].rearrange("p (m t) -> p t m", t=PACK))
 
-        def gather(dst, lst, h, s):
-            cols = slice(h * HALF // 16, (h + 1) * HALF // 16)
-            nc.vector.tensor_copy(dst[:], x[s][:].indirect(lst[:, cols]))
+        def gather(dst, lst, s, cols):
+            nc.vector.tensor_copy(dst, x[s][:].indirect(lst[:, cols.start // 16 : cols.stop // 16]))
 
-        def combine(h, s, second, cols=slice(0, HALF)):
+        def scale(h, s, cols):
             a, i = divmod(s, PACK)
-            m = larger[h, s]
-            nc.vector.tensor_tensor(m[:, cols], pick1[h, s][:, cols], second[:, cols], MAX)
-            nc.scalar.activation(u_bf[h, a][:, cols, i], m[:, cols], COPY, scale=fk_sb[:, a, i : i + 1])
+            nc.scalar.activation(u_bf[h, a][:, cols, i], larger[h][:, s, cols], COPY, scale=fk_sb[:, a, i : i + 1])
+
+        def combine_a(s0, s1):
+            nc.vector.tensor_tensor(larger[0][:, s0:s1, :], pick1[:, s0:s1, 0:HALF], pick2_a[:, s0:s1, :], MAX)
+            for s in range(s0, s1):
+                scale(0, s, slice(0, HALF))
+
+        def combine_b(s, second, cols=slice(0, HALF)):
+            nc.vector.tensor_tensor(larger[1][:, s, cols], pick1[:, s, HALF:J][:, cols], second[:, cols], MAX)
+            scale(1, s, cols)
 
         def quantise_u(key, src):
             nc.vector.quantize_mx(out=u_codes[key][:].bitcast(FP8X4), scales=u_planes[key][:], in_=src)
 
         def multiply(c, a, key, col0):
             cols = slice(col0, col0 + QUART)
+            rows = PACK // banks[c]
             for t in range(PACK):
                 nc.tensor.matmul_mx(
-                    out=acc[c][:, t, :],
+                    out=acc[c, t // rows][:, t % rows, :],
                     lhsT=w_codes[a][:, t, :].bitcast(FP8X4),
                     lhsT_scale=w_planes[4 * a : P, t, :],
                     rhs=u_codes[key][:, cols].bitcast(FP8X4),
                     rhs_scale=u_planes[key][:, cols],
-                    start=(a == 0 and t == 0),
-                    stop=(a == PASSES - 1 and t == PACK - 1),
+                    start=(a == 0 and t % rows == 0),
+                    stop=(a == PASSES - 1 and t % rows == rows - 1),
                 )
 
-        def weigh(c, pieces):
-            cols = slice(c * QUART, (c + 1) * QUART)
-            rows = PACK // pieces
-            for t in range(0, PACK, rows):
-                nc.vector.tensor_tensor(
-                    y_sb[c][:, t : t + rows, :],
-                    acc[c][:, t : t + rows, :],
-                    rw_sb[:, cols].unsqueeze(1).to_broadcast([P, rows, QUART]),
-                    MULT,
-                )
-            nc.sync.dma_start(out_rows[:, :, cols], y_sb[c][:])
-
-        def round_y(c):
-            cols = slice(c * QUART, (c + 1) * QUART)
-            nc.scalar.copy(
-                y_bf[:, cols, :].rearrange("p (c i) t -> p c t i", i=4),
-                y_sb[c][:].rearrange("p t (c i) -> p c t i", i=4),
+        def weigh(c, t0, t1, j0, j1):
+            rows = PACK // banks[c]
+            nc.vector.tensor_tensor(
+                y_sb[c][:, t0:t1, j0:j1],
+                acc[c, t0 // rows][:, t0 % rows : t0 % rows + t1 - t0, j0:j1],
+                rw_sb[:, c * QUART + j0 : c * QUART + j1].unsqueeze(1).to_broadcast([P, t1 - t0, j1 - j0]),
+                MULT,
             )
 
-        def weigh_and_round(c):
-            cols = slice(c * QUART, (c + 1) * QUART)
-            nc.vector.tensor_tensor(
-                y_bf[:, cols, :].rearrange("p (c i) t -> p c t i", i=4),
-                acc[c][:].rearrange("p t (c i) -> p c t i", i=4),
-                rw_sb[:, cols].rearrange("p (c i) -> p c i", i=4).unsqueeze(2).to_broadcast([P, QUART // 4, PACK, 4]),
-                MULT,
+        def store_y(c):
+            nc.sync.dma_start(out_rows[:, :, c * QUART : (c + 1) * QUART], y_sb[c][:])
+
+        def round_y(copy, c, j0, j1):
+            copy(
+                y_bf[:, c * QUART + j0 : c * QUART + j1, :].rearrange("p (c i) t -> p c t i", i=4),
+                y_sb[c][:, :, j0:j1].rearrange("p t (c i) -> p c t i", i=4),
             )
 
         def pack(c0, c1):
@@ -158,23 +159,29 @@ def tile_list_head_larger_inputs_pl_kernel(tc, xf, fk, w_words, w_scales, rw, of
                 in_=y_bf[:, cols, :].rearrange("p j t -> p (j t)"),
             )
 
-        for s in range(NPL):
-            gather(pick1[0, s], list1, 0, s)
-            gather(ring2[0], list2, 0, s)
-            gather(pick1[1, s], list1, 1, s)
-            combine(0, s, ring2[0])
+        half_a, half_b = slice(0, HALF), slice(HALF, J)
+        groups = [(0, 4), (4, 6), (6, 7), (7, 8)]
+        for s0, s1 in groups:
+            for s in range(s0, s1 - 1):
+                gather(pick1[:, s, :], list1, s, slice(0, J))
+                gather(pick2_a[:, s, :], list2, s, half_a)
+            s = s1 - 1
+            gather(pick1[:, s, half_a], list1, s, half_a)
+            gather(pick2_a[:, s, :], list2, s, half_a)
+            gather(pick1[:, s, half_b], list1, s, half_b)
+            combine_a(s0, s1)
         deal_w()
 
         last = NPL - 1
         order = [last] + list(range(last))
-        second = {last: ring2[1], 0: ring2[0], 1: pick1[0, last]}
+        second = {last: spare[:], 0: pick2_a[:, last, :], 1: pick1[:, last, half_a]}
         for n in range(3, last):
             second[order[n]] = second[order[n - 3]]
         second[order[last]] = second[order[last - 2]]
         for n, s in enumerate(order[:last]):
-            gather(second[s], list2, 1, s)
+            gather(second[s], list2, s, half_b)
             if n > 0:
-                combine(1, order[n - 1], second[order[n - 1]])
+                combine_b(order[n - 1], second[order[n - 1]])
             if n == 1:
                 quantise_u((0, 0), u_bf_a[:].rearrange("p a j i -> p (a j i)"))
                 for c in range(2):
@@ -184,22 +191,29 @@ def tile_list_head_larger_inputs_pl_kernel(tc, xf, fk, w_words, w_scales, rw, of
                 quantise_u((1, 0), u_bf[1, 0].rearrange("p j i -> p (j i)"))
                 for c in range(2):
                     multiply(2 + c, 0, (1, 0), c * QUART)
-        combine(1, order[last - 1], second[order[last - 1]])
-        gather(second[order[last]], list2, 1, order[last])
+        combine_b(order[last - 1], second[order[last - 1]])
+        gather(second[order[last]], list2, order[last], half_b)
         for d in range(2):
-            combine(1, order[last], second[order[last]], slice(d * QUART, (d + 1) * QUART))
+            combine_b(order[last], second[order[last]], slice(d * QUART, (d + 1) * QUART))
         for d in range(2):
             quantise_u((1, 1 + d), u_bf[1, 1][:, d * QUART : (d + 1) * QUART, :].rearrange("p j i -> p (j i)"))
             multiply(2 + d, 1, (1, 1 + d), 0)
         for c in range(2):
-            weigh(c, 2)
-            round_y(c)
+            weigh(c, 0, 2, 0, QUART)
+            weigh(c, 2, 4, 0, QUART)
+            store_y(c)
+            round_y(nc.scalar.copy, c, 0, QUART)
+        weigh(2, 0, 2, 0, QUART)
+        weigh(2, 2, 4, 0, QUART)
+        store_y(2)
+        round_y(nc.scalar.copy, 2, 0, QUART)
+        weigh(3, 0, 4, 0, QUART // 2)
+        weigh(3, 0, 4, QUART // 2, QUART)
+        store_y(3)
+        round_y(nc.vector.tensor_copy, 3, 0, QUART // 2)
+        round_y(nc.scalar.copy, 3, QUART // 2, QUART)
         pack(0, 2)
         nc.sync.dma_start(out_words[:, 0:HALF], y_codes[:, 0:HALF].bitcast(I32))
-        weigh(2, 1)
-        round_y(2)
-        weigh_and_round(3)
-        weigh(3, 1)
         pack(2, 3)
         pack(3, 4)
         nc.scalar.dma_start(out_words[:, HALF:J], y_codes[:, HALF:J].bitcast(I32))

@@ -54,16 +54,18 @@ def tile_list_head_larger_inputs_pl_kernel(tc, xf, fk, w_words, w_scales, rw, of
         nc.sync.dma_start(list1[:], offs)
         nc.sync.dma_start(list2[:], offs2)
         load_x(1)
-        nc.sync.dma_start(fk_sb[:], fk.rearrange("(a p i) o -> p a (i o)", a=PASSES, i=PACK))
-        for s in range(2, NPL):
-            load_x(s)
         for a in range(PASSES):
             load_w(a)
+        load_x(2)
+        load_x(3)
         for q in range(4):
             nc.sync.dma_start(
                 w_raw_planes[32 * q : 32 * q + 4 * PASSES, :].bitcast(I32),
                 w_scales[:, 4 * q : 4 * q + 4, :].bitcast(I32),
             )
+        nc.sync.dma_start(fk_sb[:], fk.rearrange("(a p i) o -> p a (i o)", a=PASSES, i=PACK))
+        for s in range(4, NPL):
+            load_x(s)
         nc.sync.dma_start(rw_sb[:], rw[0].partition_broadcast(P))
 
         pick1 = keep.tile([P, NPL, J], F32, name="pick1")
@@ -213,10 +215,10 @@ def tile_list_head_larger_inputs_pl_kernel(tc, xf, fk, w_words, w_scales, rw, of
         round_y(nc.vector.tensor_copy, 3, 0, QUART // 2)
         round_y(nc.scalar.copy, 3, QUART // 2, QUART)
         pack(0, 2)
-        nc.sync.dma_start(out_words[:, 0:HALF], y_codes[:, 0:HALF].bitcast(I32))
         pack(2, 3)
+        nc.sync.dma_start(out_words[:, 0 : 3 * QUART], y_codes[:, 0 : 3 * QUART].bitcast(I32))
         pack(3, 4)
-        nc.scalar.dma_start(out_words[:, HALF:J], y_codes[:, HALF:J].bitcast(I32))
+        nc.scalar.dma_start(out_words[:, 3 * QUART : J], y_codes[:, 3 * QUART : J].bitcast(I32))
         for q in range(4):
             eng = nc.sync if q % 2 == 0 else nc.scalar
             eng.dma_start(out_2[0, 4 * q : 4 * q + 4, :].bitcast(I32), y_planes[32 * q : 32 * q + 4, :].bitcast(I32))

from contextlib import ExitStack

import concourse.mybir as mybir

K, T, J, N = 1024, 1024, 512, 512
FLOPS = 2 * K * J * N

F32 = mybir.dt.float32
BF16 = mybir.dt.bfloat16
I32 = mybir.dt.int32
U32 = mybir.dt.uint32
U16 = mybir.dt.uint16
U8 = mybir.dt.uint8
FP8X4 = mybir.dt.float8_e4m3fn_x4
COPY = mybir.ActivationFunctionType.Copy
MAX = mybir.AluOpType.max
MULT = mybir.AluOpType.mult

P = 128
PACK = 4
PASSES = K // (P * PACK)
NPL = PASSES * PACK
HALF = J // 2
QUART = 128


def tile_list_head_larger_inputs_pl_kernel(tc, xf, fk, w_words, w_scales, rw, offs, offs2, out_0, out_1, out_2):
    nc = tc.nc
    with ExitStack() as ctx:
        keep = ctx.enter_context(tc.tile_pool(name="keep", bufs=1))
        psum = ctx.enter_context(tc.psum_pool(name="psum", bufs=1))

        list1 = keep.tile([P, J // 16], U16, name="list1")
        list2 = keep.tile([P, J // 16], U16, name="list2")
        x = [keep.tile([P, T], F32, name=f"x{s}") for s in range(NPL)]
        fk_sb = keep.tile([P, PASSES, PACK], F32, name="fk_sb")
        rw_sb = keep.tile([P, J], F32, name="rw_sb")
        w_raw = [keep.tile([P, N], U32, name=f"w_raw{a}") for a in range(PASSES)]
        w_raw_planes = keep.tile([P, N], U8, name="w_raw_planes")
        w_codes = [keep.tile([P, PACK, P], U32, name=f"w_codes{a}", align_bytes=64) for a in range(PASSES)]
        w_planes = keep.tile([P, PACK, P], U8, name="w_planes", align_bytes=64)

        x_rows = xf.rearrange("(a p i) t -> a i p t", a=PASSES, i=PACK)

        def load_x(s):
            nc.sync.dma_start(x[s][:], x_rows[s // PACK, s % PACK])

        def load_w(a):
            nc.sync.dma_start(w_raw[a][:].bitcast(I32), w_words[a].rearrange("p n r -> p (n r)").bitcast(I32))

        nc.vector.memset(w_raw_planes[:].bitcast(U32), 0)

        load_x(0)
        nc.sync.dma_start(list1[:], offs)
        nc.sync.dma_start(list2[:], offs2)
        load_x(1)
        for a in range(PASSES):
            load_w(a)
        load_x(2)
        load_x(3)
        for q in range(4):
            nc.sync.dma_start(
                w_raw_planes[32 * q : 32 * q + 4 * PASSES, :].bitcast(I32),
                w_scales[:, 4 * q : 4 * q + 4, :].bitcast(I32),
            )
        nc.sync.dma_start(fk_sb[:], fk.rearrange("(a p i) o -> p a (i o)", a=PASSES, i=PACK))
        for s in range(4, NPL):
            load_x(s)
        nc.sync.dma_start(rw_sb[:], rw[0].partition_broadcast(P))

        pick1 = keep.tile([P, NPL, J], F32, name="pick1")
        pick2_a = keep.tile([P, NPL, HALF], F32, name="pick2_a")
        spare = keep.tile([P, HALF], F32, name="spare")
        larger = [keep.tile([P, NPL, HALF], F32, name=f"larger{h}") for h in range(2)]
        u_bf_a = keep.tile([P, PASSES, HALF, PACK], BF16, name="u_bf_a", align_bytes=64)
        u_bf_b = [keep.tile([P, HALF, PACK], BF16, name=f"u_bf_b{a}", align_bytes=64) for a in range(PASSES)]
        u_bf = {(0, a): u_bf_a[:, a] for a in range(PASSES)}
        for a in range(PASSES):
            u_bf[1, a] = u_bf_b[a][:]
        u_codes = {}
        u_planes = {}
        for key, width in (((0, 0), 2 * HALF), ((1, 0), HALF), ((1, 1), QUART), ((1, 2), QUART)):
            u_codes[key] = keep.tile([P, width], U32, name=f"u_codes{key[0]}{key[1]}", align_bytes=64)
            u_planes[key] = keep.tile([P, width], U8, name=f"u_planes{key[0]}{key[1]}", align_bytes=64)
        banks = {0: 1, 1: 1, 2: 2, 3: 1}
        acc = {
            (c, b): psum.tile([P, PACK // banks[c], QUART], F32, name=f"acc{c}{b}") for c in range(4) for b in range(banks[c])
        }
        y_sb = [keep.tile([P, PACK, QUART], F32, name=f"y_sb{c}") for c in range(4)]
        y_bf = keep.tile([P, J, PACK], BF16, name="y_bf", align_bytes=64)
        y_codes = keep.tile([P, J], U32, name="y_codes", align_bytes=64)
        y_planes = keep.tile([P, J], U8, name="y_planes", align_bytes=64)

        out_rows = out_0.rearrange("(p t) j -> p t j", t=PACK)
        out_words = out_1[0].rearrange("p j r -> p (j r)").bitcast(I32)

        def deal_w():
            for a in range(PASSES):
                nc.gpsimd.tensor_copy(
                    w_codes[a][:].rearrange("p t (c i) -> p c t i", i=4),
                    w_raw[a][:].rearrange("p (c i t) -> p c t i", i=4, t=PACK),
                )
            nc.gpsimd.tensor_copy(w_planes[:], w_raw_planes[:].rearrange("p (m t) -> p t m", t=PACK))

        def gather(dst, lst, s, cols):
            nc.vector.tensor_copy(dst, x[s][:].indirect(lst[:, cols.start // 16 : cols.stop // 16]))

        def scale(h, s, cols):
            a, i = divmod(s, PACK)
            nc.scalar.activation(u_bf[h, a][:, cols, i], larger[h][:, s, cols], COPY, scale=fk_sb[:, a, i : i + 1])

        def combine_a(s0, s1):
            nc.vector.tensor_tensor(larger[0][:, s0:s1, :], pick1[:, s0:s1, 0:HALF], pick2_a[:, s0:s1, :], MAX)
            for s in range(s0, s1):
                scale(0, s, slice(0, HALF))

        def combine_b(s, second, cols=slice(0, HALF)):
            nc.vector.tensor_tensor(larger[1][:, s, cols], pick1[:, s, HALF:J][:, cols], second[:, cols], MAX)
            scale(1, s, cols)

        def quantise_u(key, src):
            nc.vector.quantize_mx(out=u_codes[key][:].bitcast(FP8X4), scales=u_planes[key][:], in_=src)

        def multiply(c, a, key, col0):
            cols = slice(col0, col0 + QUART)
            rows = PACK // banks[c]
            for t in range(PACK):
                nc.tensor.matmul_mx(
                    out=acc[c, t // rows][:, t % rows, :],
                    lhsT=w_codes[a][:, t, :].bitcast(FP8X4),
                    lhsT_scale=w_planes[4 * a : P, t, :],
                    rhs=u_codes[key][:, cols].bitcast(FP8X4),
                    rhs_scale=u_planes[key][:, cols],
                    start=(a == 0 and t % rows == 0),
                    stop=(a == PASSES - 1 and t % rows == rows - 1),
                )

        def weigh(c, t0, t1, j0, j1):
            rows = PACK // banks[c]
            nc.vector.tensor_tensor(
                y_sb[c][:, t0:t1, j0:j1],
                acc[c, t0 // rows][:, t0 % rows : t0 % rows + t1 - t0, j0:j1],
                rw_sb[:, c * QUART + j0 : c * QUART + j1].unsqueeze(1).to_broadcast([P, t1 - t0, j1 - j0]),
                MULT,
            )

        def store_y(c):
            nc.sync.dma_start(out_rows[:, :, c * QUART : (c + 1) * QUART], y_sb[c][:])

        def round_y(copy, c, j0, j1):
            copy(
                y_bf[:, c * QUART + j0 : c * QUART + j1, :].rearrange("p (c i) t -> p c t i", i=4),
                y_sb[c][:, :, j0:j1].rearrange("p t (c i) -> p c t i", i=4),
            )

        def pack(c0, c1):
            cols = slice(c0 * QUART, c1 * QUART)
            nc.vector.quantize_mx(
                out=y_codes[:, cols].bitcast(FP8X4),
                scales=y_planes[:, cols],
                in_=y_bf[:, cols, :].rearrange("p j t -> p (j t)"),
            )

        half_a, half_b = slice(0, HALF), slice(HALF, J)
        groups = [(0, 4), (4, 6), (6, 7), (7, 8)]
        for s0, s1 in groups:
            for s in range(s0, s1 - 1):
                gather(pick1[:, s, :], list1, s, slice(0, J))
                gather(pick2_a[:, s, :], list2, s, half_a)
            s = s1 - 1
            gather(pick1[:, s, half_a], list1, s, half_a)
            gather(pick2_a[:, s, :], list2, s, half_a)
            gather(pick1[:, s, half_b], list1, s, half_b)
            combine_a(s0, s1)
        deal_w()

        last = NPL - 1
        order = [last] + list(range(last))
        second = {last: spare[:], 0: pick2_a[:, last, :], 1: pick1[:, last, half_a]}
        for n in range(3, last):
            second[order[n]] = second[order[n - 3]]
        second[order[last]] = second[order[last - 2]]
        for n, s in enumerate(order[:last]):
            gather(second[s], list2, s, half_b)
            if n > 0:
                combine_b(order[n - 1], second[order[n - 1]])
            if n == 1:
                quantise_u((0, 0), u_bf_a[:].rearrange("p a j i -> p (a j i)"))
                for c in range(2):
                    for a in range(PASSES):
                        multiply(c, a, (0, 0), a * HALF + c * QUART)
            if n == 6:
                quantise_u((1, 0), u_bf[1, 0].rearrange("p j i -> p (j i)"))
                for c in range(2):
                    multiply(2 + c, 0, (1, 0), c * QUART)
        combine_b(order[last - 1], second[order[last - 1]])
        gather(second[order[last]], list2, order[last], half_b)
        for d in range(2):
            combine_b(order[last], second[order[last]], slice(d * QUART, (d + 1) * QUART))
        for d in range(2):
            quantise_u((1, 1 + d), u_bf[1, 1][:, d * QUART : (d + 1) * QUART, :].rearrange("p j i -> p (j i)"))
            multiply(2 + d, 1, (1, 1 + d), 0)
        for c in range(2):
            weigh(c, 0, 2, 0, QUART)
            weigh(c, 2, 4, 0, QUART)
            store_y(c)
            round_y(nc.scalar.copy, c, 0, QUART)
        weigh(2, 0, 2, 0, QUART)
        weigh(2, 2, 4, 0, QUART)
        store_y(2)
        round_y(nc.scalar.copy, 2, 0, QUART)
        weigh(3, 0, 4, 0, QUART // 2)
        weigh(3, 0, 4, QUART // 2, QUART)
        store_y(3)
        round_y(nc.vector.tensor_copy, 3, 0, QUART // 2)
        round_y(nc.scalar.copy, 3, QUART // 2, QUART)
        pack(0, 2)
        pack(2, 3)
        nc.sync.dma_start(out_words[:, 0 : 3 * QUART], y_codes[:, 0 : 3 * QUART].bitcast(I32))
        pack(3, 4)
        nc.scalar.dma_start(out_words[:, 3 * QUART : J], y_codes[:, 3 * QUART : J].bitcast(I32))
        for q in range(4):
            eng = nc.sync if q % 2 == 0 else nc.scalar
            eng.dma_start(out_2[0, 4 * q : 4 * q + 4, :].bitcast(I32), y_planes[32 * q : 32 * q + 4, :].bitcast(I32))
